import numpy as np
import ml_dtypes


def mxq(x, axis, fmt="e4m3"):
    dtype, down = {"e4m3": (ml_dtypes.float8_e4m3fn, 7), "e5m2": (ml_dtypes.float8_e5m2, 14)}[fmt]
    v = np.moveaxis(np.asarray(x, np.float32).astype(ml_dtypes.bfloat16).astype(np.float64), axis, -1)
    blocks = v.reshape(v.shape[:-1] + (-1, 32))
    amax = np.abs(blocks).max(-1, keepdims=True)
    byte = np.maximum(np.where(amax > 0, np.frexp(amax)[1] - 1 + 127, 0) - down, 1)
    scale = np.exp2(byte - 127.0)
    codes = (blocks / scale).astype(np.float32).astype(dtype).astype(np.float64)
    return np.moveaxis((codes * scale).reshape(v.shape), -1, axis)


WIDE = False


def mx_kscale(k):
    if not WIDE:
        return np.ones(k)
    levels = np.array([10, -10, 5, -5, 0])
    if k % 512:
        return np.exp2(np.random.permutation(np.resize(levels, k // 32))).repeat(32)
    a = np.empty((k // 512, 16))
    for p in range(k // 512):
        a[p, :8] = np.random.permutation(np.resize(levels, 8))
        for g in range(8):
            far = levels[np.abs(levels - a[p, g]) >= 10]
            a[p, g + 8] = far[np.random.randint(len(far))]
    return np.exp2(a.ravel()).repeat(32)


def f64(x):
    return np.asarray(x).astype(np.float64)


def striped(idx):
    return np.tile(idx.reshape(-1, 16).T, (8, 1)).astype(np.uint16)


def unstriped(offs):
    return offs[:16].T.reshape(-1).astype(np.int64)


def striped8(idx):
    return np.concatenate([x.reshape(-1, 16).T for x in idx]).astype(np.uint16)


def runs(offs, k):
    lists = np.stack([offs[16 * r : 16 * r + 16].T.reshape(-1) for r in range(8)]).astype(np.int64)
    return lists[np.arange(k) % 512 // 64]


def pack_weight(w):
    k, n = w.shape
    w = f64(np.asarray(w, np.float32).astype(ml_dtypes.bfloat16)).reshape(k // 32, 32, n)
    amax = np.abs(w).max(1)
    byte = np.clip(np.where(amax > 0, np.frexp(amax)[1] - 1 + 127 - 7, 1), 1, 254)
    scaled = (w * np.exp2(127.0 - byte)[:, None, :]).reshape(k, n).astype(np.float32)
    words = np.ascontiguousarray(scaled.reshape(k // 512, 128, 4, n).transpose(0, 1, 3, 2)).astype(ml_dtypes.float8_e4m3fn).view(np.uint8)
    return words, np.ascontiguousarray(byte.astype(np.uint8).reshape(k // 512, 16, n))


def unpack_weight(words, scales):
    g, p, n, _ = words.shape
    vals = np.ascontiguousarray(words).view(ml_dtypes.float8_e4m3fn).astype(np.float64) * np.repeat(np.exp2(scales.astype(np.float64) - 127.0), 8, axis=1)[..., None]
    return vals.transpose(0, 1, 3, 2).reshape(g * 512, n)

def planes(y):
    n, m = y.shape
    v = y.astype(np.float32).astype(ml_dtypes.bfloat16).astype(np.float64).reshape(n // 32, 32, m)
    top = np.abs(v).max(1)
    byte = np.clip(np.where(top > 0, np.frexp(top)[1] - 1 + 127 - 7, 1), 1, 254)
    codes = (v * np.exp2(127.0 - byte)[:, None, :]).reshape(n, m).astype(np.float32).astype(ml_dtypes.float8_e4m3fn).view(np.uint8)
    words = codes.reshape(n // 512, 128, 4, m).transpose(0, 1, 3, 2)
    return np.ascontiguousarray(words), np.ascontiguousarray(byte.astype(np.uint8).reshape(n // 512, 16, m))


K, T, S, V, N, H = 512, 2048, 1024, 512, 512, 512


def setup_inputs():
    n = np.random.standard_normal
    s = mx_kscale(K)[:, None]
    u = mx_kscale(H)
    packed_xT = pack_weight(n((K, T)) * s)
    packed_w1 = pack_weight(n((K, H)) / np.sqrt(K) / s)
    packed_w2 = pack_weight(n((H, N)) / np.sqrt(H) / u[:, None])
    return {
        "x_words": packed_xT[0],
        "x_scales": packed_xT[1],
        "w1_words": packed_w1[0],
        "w1_scales": packed_w1[1],
        "gn": (np.random.uniform(0.5, 1.5, (H, 1)) * u[:, None]).astype(np.float32),
        "w2_words": packed_w2[0],
        "w2_scales": packed_w2[1],
        "offs": striped(np.random.permutation(T)[:S]),
        "n1": striped8(np.stack([np.random.permutation(S) for _ in range(8)])),
        "n2": striped8(np.stack([np.random.permutation(V) for _ in range(8)])),
        "n3": striped8(np.stack([np.random.permutation(V) for _ in range(8)])),
        "n4": striped8(np.stack([np.random.permutation(V) for _ in range(8)])),
    }


def reference(x_words, x_scales, w1_words, w1_scales, gn, w2_words, w2_scales, offs, n1, n2, n3, n4):
    xq = unpack_weight(x_words, x_scales)[:, unstriped(offs)]
    y = unpack_weight(w1_words, w1_scales).T @ xq
    ln = y[np.arange(H)[:, None], runs(n1, H)]
    mx = ln.reshape(H, V, 2).max(axis=2)
    mn = ln.reshape(H, V, 2).min(axis=2)
    z = f64(gn) * (mx - (0.5 * mn))
    h = unpack_weight(w2_words, w2_scales).T @ mxq(z, 0, "e4m3")
    b1 = h[np.arange(N)[:, None], runs(n2, N)]
    b2 = h[np.arange(N)[:, None], runs(n3, N)]
    b3 = h[np.arange(N)[:, None], runs(n4, N)]
    out_0 = np.maximum(np.maximum(b1, b2), b3) - (0.5 * (np.maximum(np.minimum(b1, b2), np.minimum(np.maximum(b1, b2), b3))))
    return (out_0,) + planes(out_0)

@@ -1,0 +1,262 @@
+from contextlib import ExitStack
+
+import concourse.mybir as mybir
+from concourse.masks import make_identity
+
+K, T, S, V, N, H = 512, 2048, 1024, 512, 512, 512
+FLOPS = 2 * K * H * S + 2 * H * N * V
+
+F32 = mybir.dt.float32
+BF16 = mybir.dt.bfloat16
+I32 = mybir.dt.int32
+U32 = mybir.dt.uint32
+U16 = mybir.dt.uint16
+U8 = mybir.dt.uint8
+FP8X4 = mybir.dt.float8_e4m3fn_x4
+ALU = mybir.AluOpType
+ACT = mybir.ActivationFunctionType
+
+P = 128
+PACK = 4
+STRIPE = 16
+TOKEN_PIECES = ((0, 512), (512, 768), (768, 1024))
+PAIR_CHUNKS = ((0, 256), (256, 384), (384, 512))
+OUT_CHUNKS = ((0, 128), (128, 256), (256, 384), (384, 512))
+
+
+def load_scale_rows(nc, plane, rows):
+    for q in range(4):
+        nc.sync.dma_start(out=plane[32 * q : 32 * q + 4, :].bitcast(I32), in_=rows[4 * q : 4 * q + 4, :].bitcast(I32))
+
+
+def as_words(packed):
+    return packed[0].rearrange("p n r -> p (n r)").bitcast(I32)
+
+
+def entries(lst, start, stop):
+    return lst[:, start // STRIPE : stop // STRIPE]
+
+
+def tile_picked_laypgaptop2_none_po_kernel(
+    tc, x_words, x_scales, w1_words, w1_scales, gn, w2_words, w2_scales, offs, n1, n2, n3, n4, out_0, out_1, out_2
+):
+    nc = tc.nc
+    with ExitStack() as ctx:
+        keep = ctx.enter_context(tc.tile_pool(name="keep", bufs=1))
+        psum = ctx.enter_context(tc.psum_pool(name="psum", bufs=8))
+
+        offs_sb = keep.tile([P, S // STRIPE], U16, name="offs_sb")
+        n1_sb = keep.tile([P, S // STRIPE], U16, name="n1_sb")
+        n2_sb = keep.tile([P, V // STRIPE], U16, name="n2_sb")
+        n3_sb = keep.tile([P, V // STRIPE], U16, name="n3_sb")
+        n4_sb = keep.tile([P, V // STRIPE], U16, name="n4_sb")
+        x_codes = keep.tile([P, T], U32, name="x_codes", align_bytes=64)
+        x_plane = keep.tile([P, T], U8, name="x_plane", align_bytes=64)
+        w1_raw = keep.tile([P, H], I32, name="w1_raw", tag="slot1", align_bytes=64)
+        w2_raw = keep.tile([P, N], I32, name="w2_raw", align_bytes=64)
+        w1_plane_raw = keep.tile([P, H], U8, name="w1_plane_raw", tag="slot2", align_bytes=64)
+        w2_plane_raw = keep.tile([P, N], U8, name="w2_plane_raw", align_bytes=64)
+        gain = keep.tile([P, PACK], F32, name="gain")
+
+        nc.vector.memset(x_plane[:].bitcast(I32), 0)
+        nc.gpsimd.memset(w1_plane_raw[:].bitcast(I32), 0)
+        nc.gpsimd.memset(w2_plane_raw[:].bitcast(I32), 0)
+        identity = keep.tile([P, P], F32, name="identity")
+        make_identity(nc, identity[:])
+
+        nc.sync.dma_start(offs_sb[:], offs)
+        load_scale_rows(nc, x_plane, x_scales[0])
+        nc.sync.dma_start(n1_sb[:], n1)
+        nc.sync.dma_start(out=x_codes[:].bitcast(I32), in_=as_words(x_words))
+        nc.sync.dma_start(out=w1_raw[:], in_=as_words(w1_words))
+        load_scale_rows(nc, w1_plane_raw, w1_scales[0])
+        nc.sync.dma_start(out=gain[:], in_=gn.rearrange("(p t) o -> p (t o)", t=PACK))
+        nc.sync.dma_start(out=w2_raw[:], in_=as_words(w2_words))
+        load_scale_rows(nc, w2_plane_raw, w2_scales[0])
+        nc.sync.dma_start(n2_sb[:], n2)
+        nc.sync.dma_start(n3_sb[:], n3)
+        nc.sync.dma_start(n4_sb[:], n4)
+
+        quarter_gain = keep.tile([P, PACK], F32, name="quarter_gain")
+        gain_sign = keep.tile([P, PACK], F32, name="gain_sign")
+        nc.scalar.activation(out=quarter_gain[:], in_=gain[:], func=ACT.Copy, scale=0.25)
+        nc.scalar.activation(out=gain_sign[:], in_=gain[:], func=ACT.Sign)
+
+        picked_plane = keep.tile([P, S], U8, name="picked_plane", align_bytes=64)
+        w1_codes = keep.tile([P, H], I32, name="w1_codes", align_bytes=64)
+        w2_codes = keep.tile([P, N], I32, name="w2_codes", align_bytes=64)
+        w1_plane = keep.tile([P, H], U8, name="w1_plane", align_bytes=64)
+        w2_plane = keep.tile([P, N], U8, name="w2_plane", align_bytes=64)
+
+        def deal(dealt, raw):
+            nc.vector.tensor_copy(
+                out=dealt[:].rearrange("p (t m) -> p t m", t=PACK), in_=raw[:].rearrange("p (m t) -> p t m", t=PACK)
+            )
+
+        nc.vector.tensor_copy(out=picked_plane[:], in_=x_plane[:].indirect(offs_sb[:]))
+        picked_codes = []
+        for i, (s0, s1) in enumerate(TOKEN_PIECES):
+            piece = keep.tile([P, s1 - s0], U32, name=f"picked{i}", tag=f"slot{i}", align_bytes=64)
+            picked_codes.append(piece)
+            nc.vector.tensor_copy(out=piece[:], in_=x_codes[:].indirect(entries(offs_sb, s0, s1)))
+            if i == 0:
+                deal(w1_codes, w1_raw)
+                deal(w1_plane, w1_plane_raw)
+        deal(w2_codes, w2_raw)
+        deal(w2_plane, w2_plane_raw)
+
+        y = [keep.tile([P, S], F32, name=f"y{t}") for t in range(PACK)]
+        for t in range(PACK):
+            cols = slice(P * t, P * (t + 1))
+            for i, (s0, s1) in enumerate(TOKEN_PIECES):
+                acc = psum.tile([P, s1 - s0], F32, name="acc")
+                nc.tensor.matmul_mx(
+                    out=acc[:],
+                    lhsT=w1_codes[:, cols].bitcast(FP8X4),
+                    lhsT_scale=w1_plane[:, cols],
+                    rhs=picked_codes[i][:].bitcast(FP8X4),
+                    rhs_scale=picked_plane[:, s0:s1],
+                    start=True,
+                    stop=True,
+                )
+                nc.scalar.activation(out=y[t][:, s0:s1], in_=acc[:], func=ACT.Copy, scale=quarter_gain[:, t : t + 1])
+
+        half_h = [keep.tile([P, V], F32, name=f"half_h{t}") for t in range(PACK)]
+        for c, (v0, v1) in enumerate(PAIR_CHUNKS):
+            w = v1 - v0
+            lined = keep.tile([P, PACK, 2 * w], F32, name=f"lined{c}")
+            diff = keep.tile([P, PACK * w], F32, name=f"diff{c}")
+            total = keep.tile([P, PACK * w], F32, name=f"total{c}")
+            spread = keep.tile([P, PACK * w], F32, name=f"spread{c}")
+            signed = keep.tile([P, PACK * w], F32, name=f"signed{c}")
+            z = keep.tile([P, PACK * w], BF16, name=f"z{c}", align_bytes=64)
+            z_codes = keep.tile([P, w], U32, name=f"z_codes{c}", align_bytes=64)
+            z_plane = keep.tile([P, w], U8, name=f"z_plane{c}", align_bytes=64)
+            for t in range(PACK):
+                nc.vector.tensor_copy(out=lined[:, t, :], in_=y[t][:].indirect(entries(n1_sb, 2 * v0, 2 * v1)))
+            flat = lined[:].rearrange("p t j -> p (t j)")
+            first, second = flat[:, 0 : 2 * PACK * w : 2], flat[:, 1 : 2 * PACK * w : 2]
+            for half in (slice(0, 2 * w), slice(2 * w, 4 * w)):
+                nc.vector.tensor_tensor(out=diff[:, half], in0=first[:, half], in1=second[:, half], op=ALU.subtract)
+            nc.vector.tensor_tensor(out=total[:], in0=first, in1=second, op=ALU.add)
+            nc.scalar.activation(out=spread[:], in_=diff[:], func=ACT.Abs, scale=3.0)
+            for t in range(PACK):
+                cols = slice(w * t, w * (t + 1))
+                nc.scalar.activation(out=signed[:, cols], in_=spread[:, cols], func=ACT.Copy, scale=gain_sign[:, t : t + 1])
+            nc.vector.tensor_tensor(
+                out=z[:].rearrange("p (c i t) -> p c t i", i=2, t=PACK),
+                in0=total[:].rearrange("p (t c i) -> p c t i", i=2, t=PACK),
+                in1=signed[:].rearrange("p (t c i) -> p c t i", i=2, t=PACK),
+                op=ALU.add,
+            )
+            nc.vector.quantize_mx(out=z_codes[:].bitcast(FP8X4), scales=z_plane[:], in_=z[:])
+            for t in range(PACK):
+                cols = slice(P * t, P * (t + 1))
+                acc = psum.tile([P, w], F32, name="acc")
+                nc.tensor.matmul_mx(
+                    out=acc[:],
+                    lhsT=w2_codes[:, cols].bitcast(FP8X4),
+                    lhsT_scale=w2_plane[:, cols],
+                    rhs=z_codes[:].bitcast(FP8X4),
+                    rhs_scale=z_plane[:],
+                    start=True,
+                    stop=True,
+                )
+                nc.scalar.activation(out=half_h[t][:, v0:v1], in_=acc[:], func=ACT.Copy, scale=0.5)
+
+        out_codes = keep.tile([P, V], U32, name="out_codes", align_bytes=64)
+        out_plane = keep.tile([P, V], U8, name="out_plane", align_bytes=64)
+        out_rows = out_0.rearrange("(p t) v -> p t v", t=PACK)
+        out_words = as_words(out_1)
+        last = len(OUT_CHUNKS) - 1
+        for c, (v0, v1) in enumerate(OUT_CHUNKS):
+            w = v1 - v0
+            halves = (slice(0, 2 * w), slice(2 * w, 4 * w))
+            b1 = keep.tile([P, PACK * w], F32, name=f"b1_{c}", tag=f"after_gap{c}")
+            d = keep.tile([P, PACK * w], F32, name=f"d_{c}")
+            gap = keep.tile([P, PACK * w], F32, name=f"gap_{c}", tag=f"after_gap{c + 1}")
+            top = keep.tile([P, PACK * w], F32, name=f"top_{c}")
+            e = keep.tile([P, PACK * w], F32, name=f"e_{c}")
+            r = keep.tile([P, PACK * w], F32, name=f"r_{c}")
+            res = keep.tile([P, PACK * w], F32, name=f"res_{c}")
+            rounded = keep.tile([P, PACK * w], BF16, name=f"rounded_{c}", align_bytes=64)
+            for t in range(PACK):
+                cols = slice(w * t, w * (t + 1))
+                nc.vector.tensor_copy(out=b1[:, cols], in_=half_h[t][:].indirect(entries(n2_sb, v0, v1)))
+            for t in range(PACK):
+                cols = slice(w * t, w * (t + 1))
+                nc.vector.tensor_tensor(
+                    out=d[:, cols], in0=half_h[t][:].indirect(entries(n3_sb, v0, v1)), in1=b1[:, cols], op=ALU.subtract
+                )
+            nc.scalar.activation(out=gap[:], in_=d[:], func=ACT.Abs)
+            for half in halves:
+                nc.vector.scalar_tensor_tensor(
+                    out=top[:, half], in0=d[:, half], scalar=0.0, in1=b1[:, half], op0=ALU.max, op1=ALU.add
+                )
+            for t in range(PACK):
+                cols = slice(w * t, w * (t + 1))
+                nc.vector.tensor_tensor(
+                    out=e[:, cols], in0=half_h[t][:].indirect(entries(n4_sb, v0, v1)), in1=top[:, cols], op=ALU.subtract
+                )
+            if c < last:
+                above = keep.tile([P, PACK * w], F32, name=f"above_{c}", tag=f"after_below{c}")
+                below = keep.tile([P, PACK * w], F32, name=f"below_{c}", tag=f"after_below{c + 1}")
+                nc.scalar.activation(out=above[:], in_=e[:], func=ACT.Relu, scale=2.0)
+                for half in halves:
+                    nc.vector.scalar_tensor_tensor(
+                        out=r[:, half], in0=e[:, half], scalar=-1.0, in1=gap[:, half], op0=ALU.mult, op1=ALU.min
+                    )
+                nc.scalar.activation(out=below[:], in_=r[:], func=ACT.Relu)
+                turned = psum.tile([P, PACK * P], F32, name="acc")
+                for i, term in enumerate((top, above, below)):
+                    for t in range(PACK):
+                        nc.tensor.matmul(
+                            out=turned[:, P * t : P * (t + 1)],
+                            lhsT=term[:, P * t : P * (t + 1)],
+                            rhs=identity[:],
+                            is_transpose=True,
+                            start=(i == 0 and t == 0),
+                            stop=(i == 2 and t == PACK - 1),
+                        )
+                turned_sb = keep.tile([P, PACK * P], F32, name=f"turned_sb_{c}")
+                nc.scalar.copy(out=turned_sb[:], in_=turned[:])
+                back = psum.tile([P, PACK * P], F32, name="acc")
+                for t in range(PACK):
+                    nc.tensor.transpose(back[:, P * t : P * (t + 1)], turned_sb[:, P * t : P * (t + 1)], identity[:])
+                nc.scalar.copy(
+                    out=rounded[:].rearrange("p (c i t) -> p c t i", i=2, t=PACK),
+                    in_=back[:].rearrange("p (t c i) -> p c t i", i=2, t=PACK),
+                )
+                nc.scalar.copy(out=res[:], in_=back[:])
+                nc.vector.quantize_mx(out=out_codes[:, v0:v1].bitcast(FP8X4), scales=out_plane[:, v0:v1], in_=rounded[:])
+            else:
+                g = keep.tile([P, PACK * w], F32, name="g")
+                sides = (slice(0, w // 2), slice(w // 2, w))
+                by_tile = lambda tile, side: tile[:].rearrange("p (t v) -> p t v", t=PACK)[:, :, side]
+                for side in sides:
+                    nc.vector.scalar_tensor_tensor(
+                        out=by_tile(r, side), in0=by_tile(e, side), scalar=-1.0, in1=by_tile(gap, side), op0=ALU.mult, op1=ALU.min
+                    )
+                for side in sides:
+                    nc.vector.scalar_tensor_tensor(
+                        out=by_tile(g, side), in0=by_tile(e, side), scalar=2.0, in1=by_tile(r, side), op0=ALU.mult, op1=ALU.max
+                    )
+                for side in sides:
+                    nc.vector.tensor_tensor(out=by_tile(res, side), in0=by_tile(top, side), in1=by_tile(g, side), op=ALU.add)
+                for side in sides:
+                    nc.vector.tensor_copy(
+                        out=rounded[:, PACK * side.start : PACK * side.stop].rearrange("p (c i t) -> p c t i", i=2, t=PACK),
+                        in_=by_tile(res, side).rearrange("p t (c i) -> p c t i", i=2),
+                    )
+                for side in sides:
+                    cols = slice(v0 + side.start, v0 + side.stop)
+                    nc.vector.quantize_mx(
+                        out=out_codes[:, cols].bitcast(FP8X4),
+                        scales=out_plane[:, cols],
+                        in_=rounded[:, PACK * side.start : PACK * side.stop],
+                    )
+            nc.sync.dma_start(out=out_rows[:, :, v0:v1], in_=res[:].rearrange("p (t v) -> p t v", t=PACK))
+            nc.sync.dma_start(out=out_words[:, v0:v1], in_=out_codes[:, v0:v1].bitcast(I32))
+        for q in range(4):
+            engine = nc.sync if q % 2 else nc.scalar
+            engine.dma_start(out=out_2[0][4 * q : 4 * q + 4, :].bitcast(I32), in_=out_plane[32 * q : 32 * q + 4, :].bitcast(I32))

@@ -20,8 +20,7 @@ P = 128
 PACK = 4
 STRIPE = 16
 TOKEN_PIECES = ((0, 512), (512, 768), (768, 1024))
-PAIR_CHUNKS = ((0, 256), (256, 384), (384, 512))
-OUT_CHUNKS = ((0, 128), (128, 256), (256, 384), (384, 512))
+HIDDEN_PIECES = ((0, 256), (256, 384), (384, 512))
 
 
 def load_scale_rows(nc, plane, rows):
@@ -56,11 +55,11 @@ def tile_picked_laypgaptop2_none_po_kernel(
         w2_raw = keep.tile([P, N], I32, name="w2_raw", align_bytes=64)
         w1_plane_raw = keep.tile([P, H], U8, name="w1_plane_raw", tag="slot2", align_bytes=64)
         w2_plane_raw = keep.tile([P, N], U8, name="w2_plane_raw", align_bytes=64)
-        gain = keep.tile([P, PACK], F32, name="gain")
+        gain = keep.tile([P, H], F32, name="gain")
 
-        nc.vector.memset(x_plane[:].bitcast(I32), 0)
-        nc.gpsimd.memset(w1_plane_raw[:].bitcast(I32), 0)
-        nc.gpsimd.memset(w2_plane_raw[:].bitcast(I32), 0)
+        nc.gpsimd.memset(x_plane[:].bitcast(I32), 0)
+        nc.vector.memset(w1_plane_raw[:].bitcast(I32), 0)
+        nc.vector.memset(w2_plane_raw[:].bitcast(I32), 0)
         identity = keep.tile([P, P], F32, name="identity")
         make_identity(nc, identity[:])
 
@@ -70,17 +69,12 @@ def tile_picked_laypgaptop2_none_po_kernel(
         nc.sync.dma_start(out=x_codes[:].bitcast(I32), in_=as_words(x_words))
         nc.sync.dma_start(out=w1_raw[:], in_=as_words(w1_words))
         load_scale_rows(nc, w1_plane_raw, w1_scales[0])
-        nc.sync.dma_start(out=gain[:], in_=gn.rearrange("(p t) o -> p (t o)", t=PACK))
         nc.sync.dma_start(out=w2_raw[:], in_=as_words(w2_words))
         load_scale_rows(nc, w2_plane_raw, w2_scales[0])
+        nc.sync.dma_start(out=gain[:], in_=gn.rearrange("k o -> (k o)").partition_broadcast(P))
         nc.sync.dma_start(n2_sb[:], n2)
         nc.sync.dma_start(n3_sb[:], n3)
         nc.sync.dma_start(n4_sb[:], n4)
-
-        quarter_gain = keep.tile([P, PACK], F32, name="quarter_gain")
-        gain_sign = keep.tile([P, PACK], F32, name="gain_sign")
-        nc.scalar.activation(out=quarter_gain[:], in_=gain[:], func=ACT.Copy, scale=0.25)
-        nc.scalar.activation(out=gain_sign[:], in_=gain[:], func=ACT.Sign)
 
         picked_plane = keep.tile([P, S], U8, name="picked_plane", align_bytes=64)
         w1_codes = keep.tile([P, H], I32, name="w1_codes", align_bytes=64)
@@ -88,9 +82,10 @@ def tile_picked_laypgaptop2_none_po_kernel(
         w1_plane = keep.tile([P, H], U8, name="w1_plane", align_bytes=64)
         w2_plane = keep.tile([P, N], U8, name="w2_plane", align_bytes=64)
 
-        def deal(dealt, raw):
+        def deal(dealt, raw, run):
             nc.vector.tensor_copy(
-                out=dealt[:].rearrange("p (t m) -> p t m", t=PACK), in_=raw[:].rearrange("p (m t) -> p t m", t=PACK)
+                out=dealt[:].rearrange("p (t c i) -> p c t i", t=PACK, i=run),
+                in_=raw[:].rearrange("p (c i t) -> p c t i", t=PACK, i=run),
             )
 
         nc.vector.tensor_copy(out=picked_plane[:], in_=x_plane[:].indirect(offs_sb[:]))
@@ -100,10 +95,10 @@ def tile_picked_laypgaptop2_none_po_kernel(
             picked_codes.append(piece)
             nc.vector.tensor_copy(out=piece[:], in_=x_codes[:].indirect(entries(offs_sb, s0, s1)))
             if i == 0:
-                deal(w1_codes, w1_raw)
-                deal(w1_plane, w1_plane_raw)
-        deal(w2_codes, w2_raw)
-        deal(w2_plane, w2_plane_raw)
+                deal(w1_codes, w1_raw, 4)
+                deal(w1_plane, w1_plane_raw, 16)
+        deal(w2_codes, w2_raw, 4)
+        deal(w2_plane, w2_plane_raw, 16)
 
         y = [keep.tile([P, S], F32, name=f"y{t}") for t in range(PACK)]
         for t in range(PACK):
@@ -119,107 +114,151 @@ def tile_picked_laypgaptop2_none_po_kernel(
                     start=True,
                     stop=True,
                 )
-                nc.scalar.activation(out=y[t][:, s0:s1], in_=acc[:], func=ACT.Copy, scale=quarter_gain[:, t : t + 1])
+                nc.scalar.activation(out=y[t][:, s0:s1], in_=acc[:], func=ACT.Copy, scale=0.5)
 
         half_h = [keep.tile([P, V], F32, name=f"half_h{t}") for t in range(PACK)]
-        for c, (v0, v1) in enumerate(PAIR_CHUNKS):
-            w = v1 - v0
-            lined = keep.tile([P, PACK, 2 * w], F32, name=f"lined{c}")
-            diff = keep.tile([P, PACK * w], F32, name=f"diff{c}")
-            total = keep.tile([P, PACK * w], F32, name=f"total{c}")
-            spread = keep.tile([P, PACK * w], F32, name=f"spread{c}")
-            signed = keep.tile([P, PACK * w], F32, name=f"signed{c}")
-            z = keep.tile([P, PACK * w], BF16, name=f"z{c}", align_bytes=64)
-            z_codes = keep.tile([P, w], U32, name=f"z_codes{c}", align_bytes=64)
-            z_plane = keep.tile([P, w], U8, name=f"z_plane{c}", align_bytes=64)
+        z_codes = keep.tile([P, V], U32, name="z_codes", align_bytes=64)
+        z_plane = keep.tile([P, V], U8, name="z_plane", align_bytes=64)
+
+        def add_turned(terms):
+            bank = psum.tile([P, PACK * P], F32, name="acc")
+            for i, term in enumerate(terms):
+                for t in range(PACK):
+                    nc.tensor.matmul(
+                        out=bank[:, P * t : P * (t + 1)],
+                        lhsT=term[t],
+                        rhs=identity[:],
+                        is_transpose=True,
+                        start=(i == 0 and t == 0),
+                        stop=(i == len(terms) - 1 and t == PACK - 1),
+                    )
+            return bank
+
+        sums = []
+        for c in range(V // P):
+            v0, v1 = P * c, P * (c + 1)
+            lined = keep.tile([P, PACK, 2 * P], F32, name=f"lined{c}")
+            diff = keep.tile([P, PACK * P], F32, name=f"diff{c}")
+            lift = keep.tile([P, PACK * P], F32, name=f"lift{c}")
             for t in range(PACK):
                 nc.vector.tensor_copy(out=lined[:, t, :], in_=y[t][:].indirect(entries(n1_sb, 2 * v0, 2 * v1)))
             flat = lined[:].rearrange("p t j -> p (t j)")
-            first, second = flat[:, 0 : 2 * PACK * w : 2], flat[:, 1 : 2 * PACK * w : 2]
-            for half in (slice(0, 2 * w), slice(2 * w, 4 * w)):
-                nc.vector.tensor_tensor(out=diff[:, half], in0=first[:, half], in1=second[:, half], op=ALU.subtract)
-            nc.vector.tensor_tensor(out=total[:], in0=first, in1=second, op=ALU.add)
-            nc.scalar.activation(out=spread[:], in_=diff[:], func=ACT.Abs, scale=3.0)
-            for t in range(PACK):
-                cols = slice(w * t, w * (t + 1))
-                nc.scalar.activation(out=signed[:, cols], in_=spread[:, cols], func=ACT.Copy, scale=gain_sign[:, t : t + 1])
+            first, second = flat[:, 0 : 2 * PACK * P : 2], flat[:, 1 : 2 * PACK * P : 2]
+            for half in (slice(0, 2 * P), slice(2 * P, 4 * P)):
+                nc.vector.tensor_tensor(out=diff[:, half], in0=second[:, half], in1=first[:, half], op=ALU.subtract)
+            nc.scalar.activation(out=lift[:], in_=diff[:], func=ACT.Relu, scale=-3.0)
+            sums.append(add_turned([[term[:, P * t : P * (t + 1)] for t in range(PACK)] for term in (second, diff, lift)]))
+        for c, turned in enumerate(sums):
+            v0, v1 = P * c, P * (c + 1)
+            z_turned = keep.tile([P, H], BF16, name=f"z_turned{c}")
+            z = keep.tile([P, PACK * P], BF16, name=f"z{c}", align_bytes=64)
             nc.vector.tensor_tensor(
-                out=z[:].rearrange("p (c i t) -> p c t i", i=2, t=PACK),
-                in0=total[:].rearrange("p (t c i) -> p c t i", i=2, t=PACK),
-                in1=signed[:].rearrange("p (t c i) -> p c t i", i=2, t=PACK),
-                op=ALU.add,
+                out=z_turned[:].rearrange("v (u p e) -> v u p e", u=2, e=2),
+                in0=turned[:].rearrange("v (u e p) -> v u p e", u=2, e=2),
+                in1=gain[:].rearrange("v (p u e) -> v u p e", u=2, e=2),
+                op=ALU.mult,
             )
-            nc.vector.quantize_mx(out=z_codes[:].bitcast(FP8X4), scales=z_plane[:], in_=z[:])
-            for t in range(PACK):
-                cols = slice(P * t, P * (t + 1))
-                acc = psum.tile([P, w], F32, name="acc")
+            back = psum.tile([P, 2 * P], F32, name="acc")
+            for u in range(2):
+                nc.tensor.transpose(back[:, P * u : P * (u + 1)], z_turned[:].bitcast(F32)[:, P * u : P * (u + 1)], identity[:])
+            nc.scalar.copy(
+                out=z[:].bitcast(F32).rearrange("p (v u) -> p v u", u=2), in_=back[:].rearrange("p (u v) -> p v u", u=2)
+            )
+            nc.vector.quantize_mx(out=z_codes[:, v0:v1].bitcast(FP8X4), scales=z_plane[:, v0:v1], in_=z[:])
+        for t in range(PACK):
+            cols = slice(P * t, P * (t + 1))
+            acc = psum.tile([P, V], F32, name="acc")
+            for h0, h1 in HIDDEN_PIECES:
                 nc.tensor.matmul_mx(
-                    out=acc[:],
+                    out=acc[:, h0:h1],
                     lhsT=w2_codes[:, cols].bitcast(FP8X4),
                     lhsT_scale=w2_plane[:, cols],
-                    rhs=z_codes[:].bitcast(FP8X4),
-                    rhs_scale=z_plane[:],
+                    rhs=z_codes[:, h0:h1].bitcast(FP8X4),
+                    rhs_scale=z_plane[:, h0:h1],
                     start=True,
                     stop=True,
                 )
-                nc.scalar.activation(out=half_h[t][:, v0:v1], in_=acc[:], func=ACT.Copy, scale=0.5)
+            nc.scalar.activation(out=half_h[t][:], in_=acc[:], func=ACT.Copy, scale=0.5)
 
         out_codes = keep.tile([P, V], U32, name="out_codes", align_bytes=64)
         out_plane = keep.tile([P, V], U8, name="out_plane", align_bytes=64)
         out_rows = out_0.rearrange("(p t) v -> p t v", t=PACK)
         out_words = as_words(out_1)
-        last = len(OUT_CHUNKS) - 1
-        for c, (v0, v1) in enumerate(OUT_CHUNKS):
-            w = v1 - v0
+        w = 2 * P
+
+        def by_tile(tile, cols):
+            return tile[:].rearrange("p (t v) -> p t v", t=PACK)[:, :, cols]
+
+        def store(res, v0, v1):
+            nc.sync.dma_start(out=out_rows[:, :, v0:v1], in_=res[:].rearrange("p (t v) -> p t v", t=PACK))
+            nc.sync.dma_start(out=out_words[:, v0:v1], in_=out_codes[:, v0:v1].bitcast(I32))
+
+        for c in range(V // w):
+            v0 = w * c
             halves = (slice(0, 2 * w), slice(2 * w, 4 * w))
+            wide = w if c == 0 else P
             b1 = keep.tile([P, PACK * w], F32, name=f"b1_{c}", tag=f"after_gap{c}")
             d = keep.tile([P, PACK * w], F32, name=f"d_{c}")
-            gap = keep.tile([P, PACK * w], F32, name=f"gap_{c}", tag=f"after_gap{c + 1}")
+            if c == 0:
+                gap = keep.tile([P, PACK * w], F32, name="gap_0", tag="after_gap1")[:]
+                above = keep.tile([P, PACK * wide], F32, name="above_0")[:]
+            else:
+                both = keep.tile([P, PACK * (w + wide)], F32, name="gap_and_above", tag=f"turned_sb_0_{P}")
+                gap, above = both[:, : PACK * w], both[:, PACK * w :]
             top = keep.tile([P, PACK * w], F32, name=f"top_{c}")
-            e = keep.tile([P, PACK * w], F32, name=f"e_{c}")
             r = keep.tile([P, PACK * w], F32, name=f"r_{c}")
-            res = keep.tile([P, PACK * w], F32, name=f"res_{c}")
-            rounded = keep.tile([P, PACK * w], BF16, name=f"rounded_{c}", align_bytes=64)
             for t in range(PACK):
                 cols = slice(w * t, w * (t + 1))
-                nc.vector.tensor_copy(out=b1[:, cols], in_=half_h[t][:].indirect(entries(n2_sb, v0, v1)))
+                nc.vector.tensor_copy(out=b1[:, cols], in_=half_h[t][:].indirect(entries(n2_sb, v0, v0 + w)))
             for t in range(PACK):
                 cols = slice(w * t, w * (t + 1))
                 nc.vector.tensor_tensor(
-                    out=d[:, cols], in0=half_h[t][:].indirect(entries(n3_sb, v0, v1)), in1=b1[:, cols], op=ALU.subtract
+                    out=d[:, cols], in0=half_h[t][:].indirect(entries(n3_sb, v0, v0 + w)), in1=b1[:, cols], op=ALU.subtract
                 )
-            nc.scalar.activation(out=gap[:], in_=d[:], func=ACT.Abs)
+            nc.scalar.activation(out=gap, in_=d[:], func=ACT.Abs)
             for half in halves:
                 nc.vector.scalar_tensor_tensor(
                     out=top[:, half], in0=d[:, half], scalar=0.0, in1=b1[:, half], op0=ALU.max, op1=ALU.add
                 )
-            for t in range(PACK):
-                cols = slice(w * t, w * (t + 1))
-                nc.vector.tensor_tensor(
-                    out=e[:, cols], in0=half_h[t][:].indirect(entries(n4_sb, v0, v1)), in1=top[:, cols], op=ALU.subtract
-                )
-            if c < last:
-                above = keep.tile([P, PACK * w], F32, name=f"above_{c}", tag=f"after_below{c}")
-                below = keep.tile([P, PACK * w], F32, name=f"below_{c}", tag=f"after_below{c + 1}")
-                nc.scalar.activation(out=above[:], in_=e[:], func=ACT.Relu, scale=2.0)
-                for half in halves:
-                    nc.vector.scalar_tensor_tensor(
-                        out=r[:, half], in0=e[:, half], scalar=-1.0, in1=gap[:, half], op0=ALU.mult, op1=ALU.min
+
+            def third(c0, c1):
+                e = keep.tile([P, PACK * (c1 - c0)], F32, name=f"e_{c}_{c0}", tag=f"e_{c}")
+                for t in range(PACK):
+                    nc.vector.tensor_tensor(
+                        out=e[:, (c1 - c0) * t : (c1 - c0) * (t + 1)],
+                        in0=half_h[t][:].indirect(entries(n4_sb, v0 + c0, v0 + c1)),
+                        in1=top[:, w * t + c0 : w * t + c1],
+                        op=ALU.subtract,
                     )
-                nc.scalar.activation(out=below[:], in_=r[:], func=ACT.Relu)
-                turned = psum.tile([P, PACK * P], F32, name="acc")
-                for i, term in enumerate((top, above, below)):
-                    for t in range(PACK):
-                        nc.tensor.matmul(
-                            out=turned[:, P * t : P * (t + 1)],
-                            lhsT=term[:, P * t : P * (t + 1)],
-                            rhs=identity[:],
-                            is_transpose=True,
-                            start=(i == 0 and t == 0),
-                            stop=(i == 2 and t == PACK - 1),
-                        )
-                turned_sb = keep.tile([P, PACK * P], F32, name=f"turned_sb_{c}")
+                return e
+
+            e = third(0, wide)
+            span = slice(0, wide)
+            below = keep.tile([P, PACK * wide], F32, name=f"below_{c}")
+            nc.scalar.activation(out=above, in_=e[:], func=ACT.Relu, scale=2.0)
+            for pair in (slice(0, 2), slice(2, 4)):
+                nc.vector.scalar_tensor_tensor(
+                    out=by_tile(r, span)[:, pair],
+                    in0=by_tile(e, span)[:, pair],
+                    scalar=-1.0,
+                    in1=by_tile(gap, span)[:, pair],
+                    op0=ALU.mult,
+                    op1=ALU.min,
+                )
+            sums = []
+            for b0 in range(0, wide, P):
+                block = slice(b0, b0 + P)
+                for pair in (slice(0, 2), slice(2, 4)) if c else (slice(0, 4),):
+                    nc.scalar.activation(out=by_tile(below, block)[:, pair], in_=by_tile(r, block)[:, pair], func=ACT.Relu)
+                sums.append(add_turned([[by_tile(term, block)[:, t] for t in range(PACK)] for term in (top, above, below)]))
+            staged = []
+            for b0, turned in zip(range(0, wide, P), sums):
+                turned_sb = keep.tile([P, PACK * P], F32, name=f"turned_sb_{c}_{b0}")
                 nc.scalar.copy(out=turned_sb[:], in_=turned[:])
+                staged.append(turned_sb)
+            for b0, turned_sb in zip(range(0, wide, P), staged):
+                res = keep.tile([P, PACK * P], F32, name=f"res_{c}_{b0}")
+                rounded = keep.tile([P, PACK * P], BF16, name=f"rounded_{c}_{b0}", align_bytes=64)
                 back = psum.tile([P, PACK * P], F32, name="acc")
                 for t in range(PACK):
                     nc.tensor.transpose(back[:, P * t : P * (t + 1)], turned_sb[:, P * t : P * (t + 1)], identity[:])
@@ -228,35 +267,39 @@ def tile_picked_laypgaptop2_none_po_kernel(
                     in_=back[:].rearrange("p (t c i) -> p c t i", i=2, t=PACK),
                 )
                 nc.scalar.copy(out=res[:], in_=back[:])
-                nc.vector.quantize_mx(out=out_codes[:, v0:v1].bitcast(FP8X4), scales=out_plane[:, v0:v1], in_=rounded[:])
-            else:
-                g = keep.tile([P, PACK * w], F32, name="g")
-                sides = (slice(0, w // 2), slice(w // 2, w))
-                by_tile = lambda tile, side: tile[:].rearrange("p (t v) -> p t v", t=PACK)[:, :, side]
-                for side in sides:
-                    nc.vector.scalar_tensor_tensor(
-                        out=by_tile(r, side), in0=by_tile(e, side), scalar=-1.0, in1=by_tile(gap, side), op0=ALU.mult, op1=ALU.min
-                    )
-                for side in sides:
-                    nc.vector.scalar_tensor_tensor(
-                        out=by_tile(g, side), in0=by_tile(e, side), scalar=2.0, in1=by_tile(r, side), op0=ALU.mult, op1=ALU.max
-                    )
-                for side in sides:
-                    nc.vector.tensor_tensor(out=by_tile(res, side), in0=by_tile(top, side), in1=by_tile(g, side), op=ALU.add)
-                for side in sides:
-                    nc.vector.tensor_copy(
-                        out=rounded[:, PACK * side.start : PACK * side.stop].rearrange("p (c i t) -> p c t i", i=2, t=PACK),
-                        in_=by_tile(res, side).rearrange("p t (c i) -> p c t i", i=2),
-                    )
-                for side in sides:
-                    cols = slice(v0 + side.start, v0 + side.stop)
-                    nc.vector.quantize_mx(
-                        out=out_codes[:, cols].bitcast(FP8X4),
-                        scales=out_plane[:, cols],
-                        in_=rounded[:, PACK * side.start : PACK * side.stop],
-                    )
-            nc.sync.dma_start(out=out_rows[:, :, v0:v1], in_=res[:].rearrange("p (t v) -> p t v", t=PACK))
-            nc.sync.dma_start(out=out_words[:, v0:v1], in_=out_codes[:, v0:v1].bitcast(I32))
+                cols = slice(v0 + b0, v0 + b0 + P)
+                nc.vector.quantize_mx(out=out_codes[:, cols].bitcast(FP8X4), scales=out_plane[:, cols], in_=rounded[:])
+                store(res, cols.start, cols.stop)
+
+        e = third(P, w)
+        g = keep.tile([P, PACK * P], F32, name="g")
+        res = keep.tile([P, PACK * P], F32, name="res_last")
+        rounded = keep.tile([P, PACK * P], BF16, name="rounded_last", align_bytes=64)
+        sides = (slice(0, P // 2), slice(P // 2, P))
+        shifted = [slice(P + side.start, P + side.stop) for side in sides]
+        for side, far in zip(sides, shifted):
+            nc.vector.scalar_tensor_tensor(
+                out=by_tile(r, far), in0=by_tile(e, side), scalar=-1.0, in1=by_tile(gap, far), op0=ALU.mult, op1=ALU.min
+            )
+        for side, far in zip(sides, shifted):
+            nc.vector.scalar_tensor_tensor(
+                out=by_tile(g, side), in0=by_tile(e, side), scalar=2.0, in1=by_tile(r, far), op0=ALU.mult, op1=ALU.max
+            )
+        for side, far in zip(sides, shifted):
+            nc.vector.tensor_tensor(out=by_tile(res, side), in0=by_tile(top, far), in1=by_tile(g, side), op=ALU.add)
+        for side in sides:
+            nc.vector.tensor_copy(
+                out=rounded[:, PACK * side.start : PACK * side.stop].rearrange("p (c i t) -> p c t i", i=2, t=PACK),
+                in_=by_tile(res, side).rearrange("p t (c i) -> p c t i", i=2),
+            )
+        for side in sides:
+            cols = slice(V - P + side.start, V - P + side.stop)
+            nc.vector.quantize_mx(
+                out=out_codes[:, cols].bitcast(FP8X4),
+                scales=out_plane[:, cols],
+                in_=rounded[:, PACK * side.start : PACK * side.stop],
+            )
+        store(res, V - P, V)
         for q in range(4):
             engine = nc.sync if q % 2 else nc.scalar
             engine.dma_start(out=out_2[0][4 * q : 4 * q + 4, :].bitcast(I32), in_=out_plane[32 * q : 32 * q + 4, :].bitcast(I32))

@@ -23,9 +23,9 @@ TOKEN_PIECES = ((0, 512), (512, 768), (768, 1024))
 HIDDEN_PIECES = ((0, 256), (256, 384), (384, 512))
 
 
-def load_scale_rows(nc, plane, rows):
+def load_scale_rows(queue, plane, rows):
     for q in range(4):
-        nc.sync.dma_start(out=plane[32 * q : 32 * q + 4, :].bitcast(I32), in_=rows[4 * q : 4 * q + 4, :].bitcast(I32))
+        queue.dma_start(out=plane[32 * q : 32 * q + 4, :].bitcast(I32), in_=rows[4 * q : 4 * q + 4, :].bitcast(I32))
 
 
 def as_words(packed):
@@ -57,20 +57,20 @@ def tile_picked_laypgaptop2_none_po_kernel(
         w2_plane_raw = keep.tile([P, N], U8, name="w2_plane_raw", align_bytes=64)
         gain = keep.tile([P, H], F32, name="gain")
 
-        nc.gpsimd.memset(x_plane[:].bitcast(I32), 0)
+        nc.vector.memset(x_plane[:].bitcast(I32), 0)
         nc.vector.memset(w1_plane_raw[:].bitcast(I32), 0)
         nc.vector.memset(w2_plane_raw[:].bitcast(I32), 0)
         identity = keep.tile([P, P], F32, name="identity")
         make_identity(nc, identity[:])
 
         nc.sync.dma_start(offs_sb[:], offs)
-        load_scale_rows(nc, x_plane, x_scales[0])
+        load_scale_rows(nc.sync, x_plane, x_scales[0])
         nc.sync.dma_start(n1_sb[:], n1)
         nc.sync.dma_start(out=x_codes[:].bitcast(I32), in_=as_words(x_words))
         nc.sync.dma_start(out=w1_raw[:], in_=as_words(w1_words))
-        load_scale_rows(nc, w1_plane_raw, w1_scales[0])
+        load_scale_rows(nc.sync, w1_plane_raw, w1_scales[0])
         nc.sync.dma_start(out=w2_raw[:], in_=as_words(w2_words))
-        load_scale_rows(nc, w2_plane_raw, w2_scales[0])
+        load_scale_rows(nc.gpsimd, w2_plane_raw, w2_scales[0])
         nc.sync.dma_start(out=gain[:], in_=gn.rearrange("k o -> (k o)").partition_broadcast(P))
         nc.sync.dma_start(n2_sb[:], n2)
         nc.sync.dma_start(n3_sb[:], n3)
@@ -101,12 +101,15 @@ def tile_picked_laypgaptop2_none_po_kernel(
         deal(w2_plane, w2_plane_raw, 16)
 
         y = [keep.tile([P, S], F32, name=f"y{t}") for t in range(PACK)]
-        for t in range(PACK):
+
+        def project(t, pieces):
             cols = slice(P * t, P * (t + 1))
-            for i, (s0, s1) in enumerate(TOKEN_PIECES):
-                acc = psum.tile([P, s1 - s0], F32, name="acc")
+            start, stop = TOKEN_PIECES[pieces[0]][0], TOKEN_PIECES[pieces[-1]][1]
+            acc = psum.tile([P, stop - start], F32, name="acc")
+            for i in pieces:
+                s0, s1 = TOKEN_PIECES[i]
                 nc.tensor.matmul_mx(
-                    out=acc[:],
+                    out=acc[:, s0 - start : s1 - start],
                     lhsT=w1_codes[:, cols].bitcast(FP8X4),
                     lhsT_scale=w1_plane[:, cols],
                     rhs=picked_codes[i][:].bitcast(FP8X4),
@@ -114,7 +117,16 @@ def tile_picked_laypgaptop2_none_po_kernel(
                     start=True,
                     stop=True,
                 )
-                nc.scalar.activation(out=y[t][:, s0:s1], in_=acc[:], func=ACT.Copy, scale=0.5)
+            nc.scalar.activation(out=y[t][:, start:stop], in_=acc[:], func=ACT.Copy, scale=0.5)
+
+        project(0, (0,))
+        project(1, (0,))
+        project(0, (1,))
+        project(0, (2,))
+        project(1, (1, 2))
+        for t in range(2, PACK):
+            project(t, (0,))
+            project(t, (1, 2))
 
         half_h = [keep.tile([P, V], F32, name=f"half_h{t}") for t in range(PACK)]
         z_codes = keep.tile([P, V], U32, name="z_codes", align_bytes=64)
@@ -135,19 +147,21 @@ def tile_picked_laypgaptop2_none_po_kernel(
             return bank
 
         sums = []
-        for c in range(V // P):
-            v0, v1 = P * c, P * (c + 1)
-            lined = keep.tile([P, PACK, 2 * P], F32, name=f"lined{c}")
-            diff = keep.tile([P, PACK * P], F32, name=f"diff{c}")
-            lift = keep.tile([P, PACK * P], F32, name=f"lift{c}")
+        for c, (v0, v1) in enumerate(HIDDEN_PIECES):
+            width = v1 - v0
+            lined = keep.tile([P, PACK, 2 * width], F32, name=f"lined{c}", tag=("lined", "slot2", "lined")[c], align_bytes=64)
+            second = keep.tile([P, PACK, width], F32, name=f"second{c}")
+            diff = keep.tile([P, PACK, width], F32, name=f"diff{c}")
+            lift = keep.tile([P, PACK, width], F32, name=f"lift{c}")
             for t in range(PACK):
                 nc.vector.tensor_copy(out=lined[:, t, :], in_=y[t][:].indirect(entries(n1_sb, 2 * v0, 2 * v1)))
-            flat = lined[:].rearrange("p t j -> p (t j)")
-            first, second = flat[:, 0 : 2 * PACK * P : 2], flat[:, 1 : 2 * PACK * P : 2]
-            for half in (slice(0, 2 * P), slice(2 * P, 4 * P)):
-                nc.vector.tensor_tensor(out=diff[:, half], in0=second[:, half], in1=first[:, half], op=ALU.subtract)
+            members = lined[:].rearrange("p t (v e) -> p t v e", e=2)
+            nc.scalar.copy(out=second[:], in_=members[:, :, :, 1])
+            for pair in (slice(0, 2), slice(2, 4)):
+                nc.vector.tensor_tensor(out=diff[:, pair], in0=members[:, pair, :, 1], in1=members[:, pair, :, 0], op=ALU.subtract)
             nc.scalar.activation(out=lift[:], in_=diff[:], func=ACT.Relu, scale=-3.0)
-            sums.append(add_turned([[term[:, P * t : P * (t + 1)] for t in range(PACK)] for term in (second, diff, lift)]))
+            for b0 in range(0, width, P):
+                sums.append(add_turned([[term[:, t, b0 : b0 + P] for t in range(PACK)] for term in (second, diff, lift)]))
         for c, turned in enumerate(sums):
             v0, v1 = P * c, P * (c + 1)
             z_turned = keep.tile([P, H], BF16, name=f"z_turned{c}")
@@ -184,122 +198,135 @@ def tile_picked_laypgaptop2_none_po_kernel(
         out_plane = keep.tile([P, V], U8, name="out_plane", align_bytes=64)
         out_rows = out_0.rearrange("(p t) v -> p t v", t=PACK)
         out_words = as_words(out_1)
-        w = 2 * P
+        pairs = (slice(0, 2), slice(2, 4))
 
-        def by_tile(tile, cols):
-            return tile[:].rearrange("p (t v) -> p t v", t=PACK)[:, :, cols]
+        def work_tile(name, width, tag=None):
+            return keep.tile([P, PACK, width], F32, name=name, tag=tag or name)
 
-        def store(res, v0, v1):
-            nc.sync.dma_start(out=out_rows[:, :, v0:v1], in_=res[:].rearrange("p (t v) -> p t v", t=PACK))
+        def look_up(out, lst, v0, minus=None):
+            width = out.shape[2]
+            for t in range(PACK):
+                window = half_h[t][:].indirect(entries(lst, v0, v0 + width))
+                if minus is None:
+                    nc.vector.tensor_copy(out=out[:, t, :], in_=window)
+                else:
+                    nc.vector.tensor_tensor(out=out[:, t, :], in0=window, in1=minus[:, t, :], op=ALU.subtract)
+
+        def fused(out, in0, scalar, op0, op1, in1):
+            for pair in pairs:
+                nc.vector.scalar_tensor_tensor(out=out[:, pair], in0=in0[:, pair], scalar=scalar, in1=in1[:, pair], op0=op0, op1=op1)
+
+        def sum_turned(name, terms):
+            turned = add_turned([[term[:, t, :] for t in range(PACK)] for term in terms])
+            staged = keep.tile([P, PACK * P], F32, name=name)
+            return turned, staged
+
+        def turn_back(staged):
+            back = psum.tile([P, PACK * P], F32, name="acc")
+            for t in range(PACK):
+                nc.tensor.transpose(back[:, P * t : P * (t + 1)], staged[:, P * t : P * (t + 1)], identity[:])
+            return back
+
+        def round_block(name, back):
+            rounded = keep.tile([P, PACK * P], BF16, name=name, align_bytes=64)
+            nc.scalar.copy(
+                out=rounded[:].rearrange("p (c i t) -> p c t i", i=2, t=PACK),
+                in_=back[:].rearrange("p (t c i) -> p c t i", i=2, t=PACK),
+            )
+            return rounded
+
+        def store_block(name, back, v0, tag=None):
+            result = work_tile(name, P, tag=tag)
+            nc.scalar.copy(out=result[:].rearrange("p t v -> p (t v)"), in_=back[:])
+            nc.sync.dma_start(out=out_rows[:, :, v0 : v0 + P], in_=result[:])
+
+        def quantize_block(rounded, v0, width):
+            cols = slice(v0, v0 + width)
+            nc.vector.quantize_mx(out=out_codes[:, cols].bitcast(FP8X4), scales=out_plane[:, cols], in_=rounded)
+
+        def store_words(v0, v1):
             nc.sync.dma_start(out=out_words[:, v0:v1], in_=out_codes[:, v0:v1].bitcast(I32))
 
-        for c in range(V // w):
-            v0 = w * c
-            halves = (slice(0, 2 * w), slice(2 * w, 4 * w))
-            wide = w if c == 0 else P
-            b1 = keep.tile([P, PACK * w], F32, name=f"b1_{c}", tag=f"after_gap{c}")
-            d = keep.tile([P, PACK * w], F32, name=f"d_{c}")
-            if c == 0:
-                gap = keep.tile([P, PACK * w], F32, name="gap_0", tag="after_gap1")[:]
-                above = keep.tile([P, PACK * wide], F32, name="above_0")[:]
-            else:
-                both = keep.tile([P, PACK * (w + wide)], F32, name="gap_and_above", tag=f"turned_sb_0_{P}")
-                gap, above = both[:, : PACK * w], both[:, PACK * w :]
-            top = keep.tile([P, PACK * w], F32, name=f"top_{c}")
-            r = keep.tile([P, PACK * w], F32, name=f"r_{c}")
-            for t in range(PACK):
-                cols = slice(w * t, w * (t + 1))
-                nc.vector.tensor_copy(out=b1[:, cols], in_=half_h[t][:].indirect(entries(n2_sb, v0, v0 + w)))
-            for t in range(PACK):
-                cols = slice(w * t, w * (t + 1))
-                nc.vector.tensor_tensor(
-                    out=d[:, cols], in0=half_h[t][:].indirect(entries(n3_sb, v0, v0 + w)), in1=b1[:, cols], op=ALU.subtract
-                )
-            nc.scalar.activation(out=gap, in_=d[:], func=ACT.Abs)
-            for half in halves:
-                nc.vector.scalar_tensor_tensor(
-                    out=top[:, half], in0=d[:, half], scalar=0.0, in1=b1[:, half], op0=ALU.max, op1=ALU.add
-                )
+        b1 = work_tile("b1_01", 2 * P)
+        d = work_tile("d_01", 2 * P)
+        gap = work_tile("gap_01", 2 * P)
+        top = work_tile("top_01", 2 * P)
+        e = work_tile("e_01", 2 * P)
+        r = work_tile("r_01", 2 * P)
+        above = work_tile("above_01", 2 * P)
+        below = work_tile("below_01", 2 * P)
+        look_up(b1[:], n2_sb, 0)
+        look_up(d[:], n3_sb, 0, minus=b1[:])
+        nc.scalar.activation(out=gap[:], in_=d[:], func=ACT.Abs)
+        fused(top[:], d[:], 0.0, ALU.max, ALU.add, b1[:])
+        look_up(e[:], n4_sb, 0, minus=top[:])
+        nc.scalar.activation(out=above[:], in_=e[:], func=ACT.Relu, scale=2.0)
+        fused(r[:], e[:], -1.0, ALU.mult, ALU.min, gap[:])
+        sums = []
+        for b in range(2):
+            block = slice(P * b, P * (b + 1))
+            nc.scalar.activation(out=below[:, :, block], in_=r[:, :, block], func=ACT.Relu)
+            sums.append(sum_turned(f"staged_{b}", (top[:, :, block], above[:, :, block], below[:, :, block])))
+        for turned, staged in sums:
+            nc.scalar.copy(out=staged[:], in_=turned[:])
+        backs = [turn_back(staged) for turned, staged in sums]
 
-            def third(c0, c1):
-                e = keep.tile([P, PACK * (c1 - c0)], F32, name=f"e_{c}_{c0}", tag=f"e_{c}")
-                for t in range(PACK):
-                    nc.vector.tensor_tensor(
-                        out=e[:, (c1 - c0) * t : (c1 - c0) * (t + 1)],
-                        in0=half_h[t][:].indirect(entries(n4_sb, v0 + c0, v0 + c1)),
-                        in1=top[:, w * t + c0 : w * t + c1],
-                        op=ALU.subtract,
-                    )
-                return e
+        b1 = work_tile("b1_23", 2 * P, tag="gap_01")
+        d = work_tile("d_2", P)
+        gap = work_tile("gap_2", P, tag="staged_0")
+        top = work_tile("top_2", P)
+        e = work_tile("e_2", P)
+        r = work_tile("r_2", P)
+        above = work_tile("above_2", P, tag="staged_1")
+        below = work_tile("below_2", P)
+        look_up(b1[:], n2_sb, 2 * P)
+        look_up(d[:], n3_sb, 2 * P, minus=b1[:, :, :P])
+        rounded_0 = round_block("rounded_0", backs[0])
+        nc.scalar.activation(out=gap[:], in_=d[:], func=ACT.Abs)
+        store_block("result_0", backs[0], 0)
+        rounded_1 = round_block("rounded_1", backs[1])
+        fused(top[:], d[:], 0.0, ALU.max, ALU.add, b1[:, :, :P])
+        look_up(e[:], n4_sb, 2 * P, minus=top[:])
+        nc.scalar.activation(out=above[:], in_=e[:], func=ACT.Relu, scale=2.0)
+        fused(r[:], e[:], -1.0, ALU.mult, ALU.min, gap[:])
+        nc.scalar.activation(out=below[:], in_=r[:], func=ACT.Relu)
+        turned, staged = sum_turned("staged_2", (top[:], above[:], below[:]))
+        store_block("result_1", backs[1], P, tag="r_2")
+        quantize_block(rounded_0[:], 0, P)
+        quantize_block(rounded_1[:], P, P)
+        store_words(0, 2 * P)
+        nc.scalar.copy(out=staged[:], in_=turned[:])
+        back = turn_back(staged)
+        rounded_2 = round_block("rounded_2", back)
+        store_block("result_2", back, 2 * P)
 
-            e = third(0, wide)
-            span = slice(0, wide)
-            below = keep.tile([P, PACK * wide], F32, name=f"below_{c}")
-            nc.scalar.activation(out=above, in_=e[:], func=ACT.Relu, scale=2.0)
-            for pair in (slice(0, 2), slice(2, 4)):
-                nc.vector.scalar_tensor_tensor(
-                    out=by_tile(r, span)[:, pair],
-                    in0=by_tile(e, span)[:, pair],
-                    scalar=-1.0,
-                    in1=by_tile(gap, span)[:, pair],
-                    op0=ALU.mult,
-                    op1=ALU.min,
-                )
-            sums = []
-            for b0 in range(0, wide, P):
-                block = slice(b0, b0 + P)
-                for pair in (slice(0, 2), slice(2, 4)) if c else (slice(0, 4),):
-                    nc.scalar.activation(out=by_tile(below, block)[:, pair], in_=by_tile(r, block)[:, pair], func=ACT.Relu)
-                sums.append(add_turned([[by_tile(term, block)[:, t] for t in range(PACK)] for term in (top, above, below)]))
-            staged = []
-            for b0, turned in zip(range(0, wide, P), sums):
-                turned_sb = keep.tile([P, PACK * P], F32, name=f"turned_sb_{c}_{b0}")
-                nc.scalar.copy(out=turned_sb[:], in_=turned[:])
-                staged.append(turned_sb)
-            for b0, turned_sb in zip(range(0, wide, P), staged):
-                res = keep.tile([P, PACK * P], F32, name=f"res_{c}_{b0}")
-                rounded = keep.tile([P, PACK * P], BF16, name=f"rounded_{c}_{b0}", align_bytes=64)
-                back = psum.tile([P, PACK * P], F32, name="acc")
-                for t in range(PACK):
-                    nc.tensor.transpose(back[:, P * t : P * (t + 1)], turned_sb[:, P * t : P * (t + 1)], identity[:])
-                nc.scalar.copy(
-                    out=rounded[:].rearrange("p (c i t) -> p c t i", i=2, t=PACK),
-                    in_=back[:].rearrange("p (t c i) -> p c t i", i=2, t=PACK),
-                )
-                nc.scalar.copy(out=res[:], in_=back[:])
-                cols = slice(v0 + b0, v0 + b0 + P)
-                nc.vector.quantize_mx(out=out_codes[:, cols].bitcast(FP8X4), scales=out_plane[:, cols], in_=rounded[:])
-                store(res, cols.start, cols.stop)
-
-        e = third(P, w)
-        g = keep.tile([P, PACK * P], F32, name="g")
-        res = keep.tile([P, PACK * P], F32, name="res_last")
-        rounded = keep.tile([P, PACK * P], BF16, name="rounded_last", align_bytes=64)
+        d = work_tile("d_3", P, tag="staged_0")
+        gap = work_tile("gap_3", P, tag="below_2")
+        top = work_tile("top_3", P)
+        e = work_tile("e_3", P)
+        r = work_tile("r_3", P)
+        g = work_tile("g_3", P)
+        result = work_tile("result_3", P)
+        rounded_3 = keep.tile([P, PACK * P], BF16, name="rounded_3", align_bytes=64)
+        look_up(d[:], n3_sb, 3 * P, minus=b1[:, :, P:])
+        nc.scalar.activation(out=gap[:], in_=d[:], func=ACT.Abs)
+        fused(top[:], d[:], 0.0, ALU.max, ALU.add, b1[:, :, P:])
+        look_up(e[:], n4_sb, 3 * P, minus=top[:])
+        fused(r[:], e[:], -1.0, ALU.mult, ALU.min, gap[:])
+        fused(g[:], e[:], 2.0, ALU.mult, ALU.max, r[:])
+        quantize_block(rounded_2[:], 2 * P, P)
         sides = (slice(0, P // 2), slice(P // 2, P))
-        shifted = [slice(P + side.start, P + side.stop) for side in sides]
-        for side, far in zip(sides, shifted):
-            nc.vector.scalar_tensor_tensor(
-                out=by_tile(r, far), in0=by_tile(e, side), scalar=-1.0, in1=by_tile(gap, far), op0=ALU.mult, op1=ALU.min
-            )
-        for side, far in zip(sides, shifted):
-            nc.vector.scalar_tensor_tensor(
-                out=by_tile(g, side), in0=by_tile(e, side), scalar=2.0, in1=by_tile(r, far), op0=ALU.mult, op1=ALU.max
-            )
-        for side, far in zip(sides, shifted):
-            nc.vector.tensor_tensor(out=by_tile(res, side), in0=by_tile(top, far), in1=by_tile(g, side), op=ALU.add)
+        for side in sides:
+            nc.vector.tensor_tensor(out=result[:, :, side], in0=top[:, :, side], in1=g[:, :, side], op=ALU.add)
+        nc.sync.dma_start(out=out_rows[:, :, 3 * P :], in_=result[:])
         for side in sides:
             nc.vector.tensor_copy(
-                out=rounded[:, PACK * side.start : PACK * side.stop].rearrange("p (c i t) -> p c t i", i=2, t=PACK),
-                in_=by_tile(res, side).rearrange("p t (c i) -> p c t i", i=2),
+                out=rounded_3[:, PACK * side.start : PACK * side.stop].rearrange("p (c i t) -> p c t i", i=2, t=PACK),
+                in_=result[:, :, side].rearrange("p t (c i) -> p c t i", i=2),
             )
         for side in sides:
-            cols = slice(V - P + side.start, V - P + side.stop)
-            nc.vector.quantize_mx(
-                out=out_codes[:, cols].bitcast(FP8X4),
-                scales=out_plane[:, cols],
-                in_=rounded[:, PACK * side.start : PACK * side.stop],
-            )
-        store(res, V - P, V)
+            quantize_block(rounded_3[:, PACK * side.start : PACK * side.stop], 3 * P + side.start, P // 2)
+        store_words(2 * P, V)
         for q in range(4):
             engine = nc.sync if q % 2 else nc.scalar
             engine.dma_start(out=out_2[0][4 * q : 4 * q + 4, :].bitcast(I32), in_=out_plane[32 * q : 32 * q + 4, :].bitcast(I32))

@@ -20,12 +20,13 @@ P = 128
 PACK = 4
 STRIPE = 16
 TOKEN_PIECES = ((0, 512), (512, 768), (768, 1024))
+PAIR_CHUNKS = ((0, 384), (384, 512))
 HIDDEN_PIECES = ((0, 256), (256, 384), (384, 512))
 
 
-def load_scale_rows(queue, plane, rows):
+def load_scale_rows(nc, plane, rows):
     for q in range(4):
-        queue.dma_start(out=plane[32 * q : 32 * q + 4, :].bitcast(I32), in_=rows[4 * q : 4 * q + 4, :].bitcast(I32))
+        nc.sync.dma_start(out=plane[32 * q : 32 * q + 4, :].bitcast(I32), in_=rows[4 * q : 4 * q + 4, :].bitcast(I32))
 
 
 def as_words(packed):
@@ -55,7 +56,7 @@ def tile_picked_laypgaptop2_none_po_kernel(
         w2_raw = keep.tile([P, N], I32, name="w2_raw", align_bytes=64)
         w1_plane_raw = keep.tile([P, H], U8, name="w1_plane_raw", tag="slot2", align_bytes=64)
         w2_plane_raw = keep.tile([P, N], U8, name="w2_plane_raw", align_bytes=64)
-        gain = keep.tile([P, H], F32, name="gain")
+        gain = keep.tile([P, PACK], F32, name="gain")
 
         nc.vector.memset(x_plane[:].bitcast(I32), 0)
         nc.vector.memset(w1_plane_raw[:].bitcast(I32), 0)
@@ -64,17 +65,22 @@ def tile_picked_laypgaptop2_none_po_kernel(
         make_identity(nc, identity[:])
 
         nc.sync.dma_start(offs_sb[:], offs)
-        load_scale_rows(nc.sync, x_plane, x_scales[0])
+        load_scale_rows(nc, x_plane, x_scales[0])
         nc.sync.dma_start(n1_sb[:], n1)
         nc.sync.dma_start(out=x_codes[:].bitcast(I32), in_=as_words(x_words))
         nc.sync.dma_start(out=w1_raw[:], in_=as_words(w1_words))
-        load_scale_rows(nc.sync, w1_plane_raw, w1_scales[0])
+        load_scale_rows(nc, w1_plane_raw, w1_scales[0])
+        nc.sync.dma_start(out=gain[:], in_=gn.rearrange("(p t) o -> p (t o)", t=PACK))
         nc.sync.dma_start(out=w2_raw[:], in_=as_words(w2_words))
-        load_scale_rows(nc.gpsimd, w2_plane_raw, w2_scales[0])
-        nc.sync.dma_start(out=gain[:], in_=gn.rearrange("k o -> (k o)").partition_broadcast(P))
+        load_scale_rows(nc, w2_plane_raw, w2_scales[0])
         nc.sync.dma_start(n2_sb[:], n2)
         nc.sync.dma_start(n3_sb[:], n3)
         nc.sync.dma_start(n4_sb[:], n4)
+
+        quarter_gain = keep.tile([P, PACK], F32, name="quarter_gain")
+        gain_sign = keep.tile([P, PACK], F32, name="gain_sign")
+        nc.scalar.activation(out=quarter_gain[:], in_=gain[:], func=ACT.Copy, scale=0.25)
+        nc.scalar.activation(out=gain_sign[:], in_=gain[:], func=ACT.Sign)
 
         picked_plane = keep.tile([P, S], U8, name="picked_plane", align_bytes=64)
         w1_codes = keep.tile([P, H], I32, name="w1_codes", align_bytes=64)
@@ -117,14 +123,11 @@ def tile_picked_laypgaptop2_none_po_kernel(
                     start=True,
                     stop=True,
                 )
-            nc.scalar.activation(out=y[t][:, start:stop], in_=acc[:], func=ACT.Copy, scale=0.5)
+            nc.scalar.activation(out=y[t][:, start:stop], in_=acc[:], func=ACT.Copy, scale=quarter_gain[:, t : t + 1])
 
-        project(0, (0,))
-        project(1, (0,))
-        project(0, (1,))
-        project(0, (2,))
-        project(1, (1, 2))
-        for t in range(2, PACK):
+        for i in range(len(TOKEN_PIECES)):
+            project(0, (i,))
+        for t in range(1, PACK):
             project(t, (0,))
             project(t, (1, 2))
 
@@ -146,39 +149,36 @@ def tile_picked_laypgaptop2_none_po_kernel(
                     )
             return bank
 
-        sums = []
-        for c, (v0, v1) in enumerate(HIDDEN_PIECES):
-            width = v1 - v0
-            lined = keep.tile([P, PACK, 2 * width], F32, name=f"lined{c}", tag=("lined", "slot2", "lined")[c], align_bytes=64)
-            second = keep.tile([P, PACK, width], F32, name=f"second{c}")
-            diff = keep.tile([P, PACK, width], F32, name=f"diff{c}")
-            lift = keep.tile([P, PACK, width], F32, name=f"lift{c}")
+        z = keep.tile([P, PACK * V], BF16, name="z", align_bytes=64)
+        for c, (v0, v1) in enumerate(PAIR_CHUNKS):
+            w = v1 - v0
+            lined = keep.tile([P, PACK, 2 * w], F32, name=f"lined{c}", tag="lined")
+            diff = keep.tile([P, PACK * w], F32, name=f"diff{c}")
+            total = keep.tile([P, PACK * w], F32, name=f"total{c}")
+            spread = keep.tile([P, PACK * w], F32, name=f"spread{c}", tag="spread")
+            signed = keep.tile([P, PACK * w], F32, name=f"signed{c}")
             for t in range(PACK):
                 nc.vector.tensor_copy(out=lined[:, t, :], in_=y[t][:].indirect(entries(n1_sb, 2 * v0, 2 * v1)))
-            members = lined[:].rearrange("p t (v e) -> p t v e", e=2)
-            nc.scalar.copy(out=second[:], in_=members[:, :, :, 1])
-            for pair in (slice(0, 2), slice(2, 4)):
-                nc.vector.tensor_tensor(out=diff[:, pair], in0=members[:, pair, :, 1], in1=members[:, pair, :, 0], op=ALU.subtract)
-            nc.scalar.activation(out=lift[:], in_=diff[:], func=ACT.Relu, scale=-3.0)
-            for b0 in range(0, width, P):
-                sums.append(add_turned([[term[:, t, b0 : b0 + P] for t in range(PACK)] for term in (second, diff, lift)]))
-        for c, turned in enumerate(sums):
-            v0, v1 = P * c, P * (c + 1)
-            z_turned = keep.tile([P, H], BF16, name=f"z_turned{c}")
-            z = keep.tile([P, PACK * P], BF16, name=f"z{c}", align_bytes=64)
+            flat = lined[:].rearrange("p t j -> p (t j)")
+            first, second = flat[:, 0 : 2 * PACK * w : 2], flat[:, 1 : 2 * PACK * w : 2]
+            for half in (slice(0, 2 * w), slice(2 * w, 4 * w)):
+                nc.vector.tensor_tensor(out=diff[:, half], in0=first[:, half], in1=second[:, half], op=ALU.subtract)
+            nc.vector.tensor_tensor(out=total[:], in0=first, in1=second, op=ALU.add)
+            nc.scalar.activation(out=spread[:], in_=diff[:], func=ACT.Abs, scale=3.0)
+            for t in range(PACK):
+                cols = slice(w * t, w * (t + 1))
+                nc.scalar.activation(out=signed[:, cols], in_=spread[:, cols], func=ACT.Copy, scale=gain_sign[:, t : t + 1])
             nc.vector.tensor_tensor(
-                out=z_turned[:].rearrange("v (u p e) -> v u p e", u=2, e=2),
-                in0=turned[:].rearrange("v (u e p) -> v u p e", u=2, e=2),
-                in1=gain[:].rearrange("v (p u e) -> v u p e", u=2, e=2),
-                op=ALU.mult,
+                out=z[:, PACK * v0 : PACK * v1].rearrange("p (c i t) -> p c t i", i=2, t=PACK),
+                in0=total[:].rearrange("p (t c i) -> p c t i", i=2, t=PACK),
+                in1=signed[:].rearrange("p (t c i) -> p c t i", i=2, t=PACK),
+                op=ALU.add,
             )
-            back = psum.tile([P, 2 * P], F32, name="acc")
-            for u in range(2):
-                nc.tensor.transpose(back[:, P * u : P * (u + 1)], z_turned[:].bitcast(F32)[:, P * u : P * (u + 1)], identity[:])
-            nc.scalar.copy(
-                out=z[:].bitcast(F32).rearrange("p (v u) -> p v u", u=2), in_=back[:].rearrange("p (u v) -> p v u", u=2)
-            )
-            nc.vector.quantize_mx(out=z_codes[:, v0:v1].bitcast(FP8X4), scales=z_plane[:, v0:v1], in_=z[:])
+            for h0, h1 in HIDDEN_PIECES:
+                if v0 <= h0 < v1:
+                    nc.vector.quantize_mx(
+                        out=z_codes[:, h0:h1].bitcast(FP8X4), scales=z_plane[:, h0:h1], in_=z[:, PACK * h0 : PACK * h1]
+                    )
         for t in range(PACK):
             cols = slice(P * t, P * (t + 1))
             acc = psum.tile([P, V], F32, name="acc")

from contextlib import ExitStack

import concourse.mybir as mybir
from concourse.masks import make_identity

K, T, S, V, N, H = 512, 2048, 1024, 512, 512, 512
FLOPS = 2 * K * H * S + 2 * H * N * V

F32 = mybir.dt.float32
BF16 = mybir.dt.bfloat16
I32 = mybir.dt.int32
U32 = mybir.dt.uint32
U16 = mybir.dt.uint16
U8 = mybir.dt.uint8
FP8X4 = mybir.dt.float8_e4m3fn_x4
ALU = mybir.AluOpType
ACT = mybir.ActivationFunctionType

P = 128
PACK = 4
STRIPE = 16
TOKEN_PIECES = ((0, 512), (512, 768), (768, 1024))
PAIR_CHUNKS = ((0, 384), (384, 512))
HIDDEN_PIECES = ((0, 256), (256, 384), (384, 512))


def load_scale_rows(nc, plane, rows):
    for q in range(4):
        nc.sync.dma_start(out=plane[32 * q : 32 * q + 4, :].bitcast(I32), in_=rows[4 * q : 4 * q + 4, :].bitcast(I32))


def as_words(packed):
    return packed[0].rearrange("p n r -> p (n r)").bitcast(I32)


def entries(lst, start, stop):
    return lst[:, start // STRIPE : stop // STRIPE]


def tile_picked_laypgaptop2_none_po_kernel(
    tc, x_words, x_scales, w1_words, w1_scales, gn, w2_words, w2_scales, offs, n1, n2, n3, n4, out_0, out_1, out_2
):
    nc = tc.nc
    with ExitStack() as ctx:
        keep = ctx.enter_context(tc.tile_pool(name="keep", bufs=1))
        psum = ctx.enter_context(tc.psum_pool(name="psum", bufs=8))

        offs_sb = keep.tile([P, S // STRIPE], U16, name="offs_sb")
        n1_sb = keep.tile([P, S // STRIPE], U16, name="n1_sb")
        n2_sb = keep.tile([P, V // STRIPE], U16, name="n2_sb")
        n3_sb = keep.tile([P, V // STRIPE], U16, name="n3_sb")
        n4_sb = keep.tile([P, V // STRIPE], U16, name="n4_sb")
        x_codes = keep.tile([P, T], U32, name="x_codes", align_bytes=64)
        x_plane = keep.tile([P, T], U8, name="x_plane", align_bytes=64)
        w1_raw = keep.tile([P, H], I32, name="w1_raw", tag="slot1", align_bytes=64)
        w2_raw = keep.tile([P, N], I32, name="w2_raw", align_bytes=64)
        w1_plane_raw = keep.tile([P, H], U8, name="w1_plane_raw", tag="slot2", align_bytes=64)
        w2_plane_raw = keep.tile([P, N], U8, name="w2_plane_raw", align_bytes=64)
        gain = keep.tile([P, PACK], F32, name="gain")

        nc.vector.memset(x_plane[:].bitcast(I32), 0)
        nc.vector.memset(w1_plane_raw[:].bitcast(I32), 0)
        nc.vector.memset(w2_plane_raw[:].bitcast(I32), 0)
        identity = keep.tile([P, P], F32, name="identity")
        make_identity(nc, identity[:])

        nc.sync.dma_start(offs_sb[:], offs)
        load_scale_rows(nc, x_plane, x_scales[0])
        nc.sync.dma_start(n1_sb[:], n1)
        nc.sync.dma_start(out=x_codes[:].bitcast(I32), in_=as_words(x_words))
        nc.sync.dma_start(out=w1_raw[:], in_=as_words(w1_words))
        load_scale_rows(nc, w1_plane_raw, w1_scales[0])
        nc.sync.dma_start(out=gain[:], in_=gn.rearrange("(p t) o -> p (t o)", t=PACK))
        nc.sync.dma_start(out=w2_raw[:], in_=as_words(w2_words))
        load_scale_rows(nc, w2_plane_raw, w2_scales[0])
        nc.sync.dma_start(n2_sb[:], n2)
        nc.sync.dma_start(n3_sb[:], n3)
        nc.sync.dma_start(n4_sb[:], n4)

        quarter_gain = keep.tile([P, PACK], F32, name="quarter_gain")
        gain_sign = keep.tile([P, PACK], F32, name="gain_sign")
        nc.scalar.activation(out=quarter_gain[:], in_=gain[:], func=ACT.Copy, scale=0.25)
        nc.scalar.activation(out=gain_sign[:], in_=gain[:], func=ACT.Sign)

        picked_plane = keep.tile([P, S], U8, name="picked_plane", align_bytes=64)
        w1_codes = keep.tile([P, H], I32, name="w1_codes", align_bytes=64)
        w2_codes = keep.tile([P, N], I32, name="w2_codes", align_bytes=64)
        w1_plane = keep.tile([P, H], U8, name="w1_plane", align_bytes=64)
        w2_plane = keep.tile([P, N], U8, name="w2_plane", align_bytes=64)

        def deal(dealt, raw, run):
            nc.vector.tensor_copy(
                out=dealt[:].rearrange("p (t c i) -> p c t i", t=PACK, i=run),
                in_=raw[:].rearrange("p (c i t) -> p c t i", t=PACK, i=run),
            )

        nc.vector.tensor_copy(out=picked_plane[:], in_=x_plane[:].indirect(offs_sb[:]))
        picked_codes = []
        for i, (s0, s1) in enumerate(TOKEN_PIECES):
            piece = keep.tile([P, s1 - s0], U32, name=f"picked{i}", tag=f"slot{i}", align_bytes=64)
            picked_codes.append(piece)
            nc.vector.tensor_copy(out=piece[:], in_=x_codes[:].indirect(entries(offs_sb, s0, s1)))
            if i == 0:
                deal(w1_codes, w1_raw, 4)
                deal(w1_plane, w1_plane_raw, 16)
        deal(w2_codes, w2_raw, 4)
        deal(w2_plane, w2_plane_raw, 16)

        y = [keep.tile([P, S], F32, name=f"y{t}") for t in range(PACK)]

        def project(t, pieces):
            cols = slice(P * t, P * (t + 1))
            start, stop = TOKEN_PIECES[pieces[0]][0], TOKEN_PIECES[pieces[-1]][1]
            acc = psum.tile([P, stop - start], F32, name="acc")
            for i in pieces:
                s0, s1 = TOKEN_PIECES[i]
                nc.tensor.matmul_mx(
                    out=acc[:, s0 - start : s1 - start],
                    lhsT=w1_codes[:, cols].bitcast(FP8X4),
                    lhsT_scale=w1_plane[:, cols],
                    rhs=picked_codes[i][:].bitcast(FP8X4),
                    rhs_scale=picked_plane[:, s0:s1],
                    start=True,
                    stop=True,
                )
            nc.scalar.activation(out=y[t][:, start:stop], in_=acc[:], func=ACT.Copy, scale=quarter_gain[:, t : t + 1])

        for i in range(len(TOKEN_PIECES)):
            project(0, (i,))
        for t in range(1, PACK):
            project(t, (0,))
            project(t, (1, 2))

        half_h = [keep.tile([P, V], F32, name=f"half_h{t}") for t in range(PACK)]
        z_codes = keep.tile([P, V], U32, name="z_codes", align_bytes=64)
        z_plane = keep.tile([P, V], U8, name="z_plane", align_bytes=64)

        def add_turned(terms):
            bank = psum.tile([P, PACK * P], F32, name="acc")
            for i, term in enumerate(terms):
                for t in range(PACK):
                    nc.tensor.matmul(
                        out=bank[:, P * t : P * (t + 1)],
                        lhsT=term[t],
                        rhs=identity[:],
                        is_transpose=True,
                        start=(i == 0 and t == 0),
                        stop=(i == len(terms) - 1 and t == PACK - 1),
                    )
            return bank

        z = keep.tile([P, PACK * V], BF16, name="z", align_bytes=64)
        for c, (v0, v1) in enumerate(PAIR_CHUNKS):
            w = v1 - v0
            lined = keep.tile([P, PACK, 2 * w], F32, name=f"lined{c}", tag="lined")
            diff = keep.tile([P, PACK * w], F32, name=f"diff{c}")
            total = keep.tile([P, PACK * w], F32, name=f"total{c}")
            spread = keep.tile([P, PACK * w], F32, name=f"spread{c}", tag="spread")
            signed = keep.tile([P, PACK * w], F32, name=f"signed{c}")
            for t in range(PACK):
                nc.vector.tensor_copy(out=lined[:, t, :], in_=y[t][:].indirect(entries(n1_sb, 2 * v0, 2 * v1)))
            flat = lined[:].rearrange("p t j -> p (t j)")
            first, second = flat[:, 0 : 2 * PACK * w : 2], flat[:, 1 : 2 * PACK * w : 2]
            for half in (slice(0, 2 * w), slice(2 * w, 4 * w)):
                nc.vector.tensor_tensor(out=diff[:, half], in0=first[:, half], in1=second[:, half], op=ALU.subtract)
            nc.vector.tensor_tensor(out=total[:], in0=first, in1=second, op=ALU.add)
            nc.scalar.activation(out=spread[:], in_=diff[:], func=ACT.Abs, scale=3.0)
            for t in range(PACK):
                cols = slice(w * t, w * (t + 1))
                nc.scalar.activation(out=signed[:, cols], in_=spread[:, cols], func=ACT.Copy, scale=gain_sign[:, t : t + 1])
            nc.vector.tensor_tensor(
                out=z[:, PACK * v0 : PACK * v1].rearrange("p (c i t) -> p c t i", i=2, t=PACK),
                in0=total[:].rearrange("p (t c i) -> p c t i", i=2, t=PACK),
                in1=signed[:].rearrange("p (t c i) -> p c t i", i=2, t=PACK),
                op=ALU.add,
            )
            for h0, h1 in HIDDEN_PIECES:
                if v0 <= h0 < v1:
                    nc.vector.quantize_mx(
                        out=z_codes[:, h0:h1].bitcast(FP8X4), scales=z_plane[:, h0:h1], in_=z[:, PACK * h0 : PACK * h1]
                    )
        for t in range(PACK):
            cols = slice(P * t, P * (t + 1))
            acc = psum.tile([P, V], F32, name="acc")
            for h0, h1 in HIDDEN_PIECES:
                nc.tensor.matmul_mx(
                    out=acc[:, h0:h1],
                    lhsT=w2_codes[:, cols].bitcast(FP8X4),
                    lhsT_scale=w2_plane[:, cols],
                    rhs=z_codes[:, h0:h1].bitcast(FP8X4),
                    rhs_scale=z_plane[:, h0:h1],
                    start=True,
                    stop=True,
                )
            nc.scalar.activation(out=half_h[t][:], in_=acc[:], func=ACT.Copy, scale=0.5)

        out_codes = keep.tile([P, V], U32, name="out_codes", align_bytes=64)
        out_plane = keep.tile([P, V], U8, name="out_plane", align_bytes=64)
        out_rows = out_0.rearrange("(p t) v -> p t v", t=PACK)
        out_words = as_words(out_1)
        pairs = (slice(0, 2), slice(2, 4))

        def work_tile(name, width, tag=None):
            return keep.tile([P, PACK, width], F32, name=name, tag=tag or name)

        def look_up(out, lst, v0, minus=None):
            width = out.shape[2]
            for t in range(PACK):
                window = half_h[t][:].indirect(entries(lst, v0, v0 + width))
                if minus is None:
                    nc.vector.tensor_copy(out=out[:, t, :], in_=window)
                else:
                    nc.vector.tensor_tensor(out=out[:, t, :], in0=window, in1=minus[:, t, :], op=ALU.subtract)

        def fused(out, in0, scalar, op0, op1, in1):
            for pair in pairs:
                nc.vector.scalar_tensor_tensor(out=out[:, pair], in0=in0[:, pair], scalar=scalar, in1=in1[:, pair], op0=op0, op1=op1)

        def sum_turned(name, terms):
            turned = add_turned([[term[:, t, :] for t in range(PACK)] for term in terms])
            staged = keep.tile([P, PACK * P], F32, name=name)
            return turned, staged

        def turn_back(staged):
            back = psum.tile([P, PACK * P], F32, name="acc")
            for t in range(PACK):
                nc.tensor.transpose(back[:, P * t : P * (t + 1)], staged[:, P * t : P * (t + 1)], identity[:])
            return back

        def round_block(name, back):
            rounded = keep.tile([P, PACK * P], BF16, name=name, align_bytes=64)
            nc.scalar.copy(
                out=rounded[:].rearrange("p (c i t) -> p c t i", i=2, t=PACK),
                in_=back[:].rearrange("p (t c i) -> p c t i", i=2, t=PACK),
            )
            return rounded

        def store_block(name, back, v0, tag=None):
            result = work_tile(name, P, tag=tag)
            nc.scalar.copy(out=result[:].rearrange("p t v -> p (t v)"), in_=back[:])
            nc.sync.dma_start(out=out_rows[:, :, v0 : v0 + P], in_=result[:])

        def quantize_block(rounded, v0, width):
            cols = slice(v0, v0 + width)
            nc.vector.quantize_mx(out=out_codes[:, cols].bitcast(FP8X4), scales=out_plane[:, cols], in_=rounded)

        def store_words(v0, v1):
            nc.sync.dma_start(out=out_words[:, v0:v1], in_=out_codes[:, v0:v1].bitcast(I32))

        b1 = work_tile("b1_01", 2 * P)
        d = work_tile("d_01", 2 * P)
        gap = work_tile("gap_01", 2 * P)
        top = work_tile("top_01", 2 * P)
        e = work_tile("e_01", 2 * P)
        r = work_tile("r_01", 2 * P)
        above = work_tile("above_01", 2 * P)
        below = work_tile("below_01", 2 * P)
        look_up(b1[:], n2_sb, 0)
        look_up(d[:], n3_sb, 0, minus=b1[:])
        nc.scalar.activation(out=gap[:], in_=d[:], func=ACT.Abs)
        fused(top[:], d[:], 0.0, ALU.max, ALU.add, b1[:])
        look_up(e[:], n4_sb, 0, minus=top[:])
        nc.scalar.activation(out=above[:], in_=e[:], func=ACT.Relu, scale=2.0)
        fused(r[:], e[:], -1.0, ALU.mult, ALU.min, gap[:])
        sums = []
        for b in range(2):
            block = slice(P * b, P * (b + 1))
            nc.scalar.activation(out=below[:, :, block], in_=r[:, :, block], func=ACT.Relu)
            sums.append(sum_turned(f"staged_{b}", (top[:, :, block], above[:, :, block], below[:, :, block])))
        for turned, staged in sums:
            nc.scalar.copy(out=staged[:], in_=turned[:])
        backs = [turn_back(staged) for turned, staged in sums]

        b1 = work_tile("b1_23", 2 * P, tag="gap_01")
        d = work_tile("d_2", P)
        gap = work_tile("gap_2", P, tag="staged_0")
        top = work_tile("top_2", P)
        e = work_tile("e_2", P)
        r = work_tile("r_2", P)
        above = work_tile("above_2", P, tag="staged_1")
        below = work_tile("below_2", P)
        look_up(b1[:], n2_sb, 2 * P)
        look_up(d[:], n3_sb, 2 * P, minus=b1[:, :, :P])
        rounded_0 = round_block("rounded_0", backs[0])
        nc.scalar.activation(out=gap[:], in_=d[:], func=ACT.Abs)
        store_block("result_0", backs[0], 0)
        rounded_1 = round_block("rounded_1", backs[1])
        fused(top[:], d[:], 0.0, ALU.max, ALU.add, b1[:, :, :P])
        look_up(e[:], n4_sb, 2 * P, minus=top[:])
        nc.scalar.activation(out=above[:], in_=e[:], func=ACT.Relu, scale=2.0)
        fused(r[:], e[:], -1.0, ALU.mult, ALU.min, gap[:])
        nc.scalar.activation(out=below[:], in_=r[:], func=ACT.Relu)
        turned, staged = sum_turned("staged_2", (top[:], above[:], below[:]))
        store_block("result_1", backs[1], P, tag="r_2")
        quantize_block(rounded_0[:], 0, P)
        quantize_block(rounded_1[:], P, P)
        store_words(0, 2 * P)
        nc.scalar.copy(out=staged[:], in_=turned[:])
        back = turn_back(staged)
        rounded_2 = round_block("rounded_2", back)
        store_block("result_2", back, 2 * P)

        d = work_tile("d_3", P, tag="staged_0")
        gap = work_tile("gap_3", P, tag="below_2")
        top = work_tile("top_3", P)
        e = work_tile("e_3", P)
        r = work_tile("r_3", P)
        g = work_tile("g_3", P)
        result = work_tile("result_3", P)
        rounded_3 = keep.tile([P, PACK * P], BF16, name="rounded_3", align_bytes=64)
        look_up(d[:], n3_sb, 3 * P, minus=b1[:, :, P:])
        nc.scalar.activation(out=gap[:], in_=d[:], func=ACT.Abs)
        fused(top[:], d[:], 0.0, ALU.max, ALU.add, b1[:, :, P:])
        look_up(e[:], n4_sb, 3 * P, minus=top[:])
        fused(r[:], e[:], -1.0, ALU.mult, ALU.min, gap[:])
        fused(g[:], e[:], 2.0, ALU.mult, ALU.max, r[:])
        quantize_block(rounded_2[:], 2 * P, P)
        sides = (slice(0, P // 2), slice(P // 2, P))
        for side in sides:
            nc.vector.tensor_tensor(out=result[:, :, side], in0=top[:, :, side], in1=g[:, :, side], op=ALU.add)
        nc.sync.dma_start(out=out_rows[:, :, 3 * P :], in_=result[:])
        for side in sides:
            nc.vector.tensor_copy(
                out=rounded_3[:, PACK * side.start : PACK * side.stop].rearrange("p (c i t) -> p c t i", i=2, t=PACK),
                in_=result[:, :, side].rearrange("p t (c i) -> p c t i", i=2),
            )
        for side in sides:
            quantize_block(rounded_3[:, PACK * side.start : PACK * side.stop], 3 * P + side.start, P // 2)
        store_words(2 * P, V)
        for q in range(4):
            engine = nc.sync if q % 2 else nc.scalar
            engine.dma_start(out=out_2[0][4 * q : 4 * q + 4, :].bitcast(I32), in_=out_plane[32 * q : 32 * q + 4, :].bitcast(I32))
